import numpy as np, ml_dtypes
CORES = [36,164,52,180,100,228,116,244]
N = 8
F = 512
GROUPS = [[0,1,2,3],[4,5,6,7]]
def setup_inputs(rng):
    return {"x": rng.standard_normal((N, 128, F), dtype=np.float32).astype(ml_dtypes.bfloat16), "w": (rng.standard_normal((N, 128, 128), dtype=np.float32) / 11).astype(ml_dtypes.bfloat16)}
def setup_inputs_big(rng):
    d = setup_inputs(rng)
    for k in ("x", "w"): d[k] = (d[k].astype(np.float32) * 1024.0).astype(d[k].dtype)
    return d
def setup_inputs_small(rng):
    d = setup_inputs(rng)
    for k in ("x", "w"): d[k] = (d[k].astype(np.float32) * (1 / 1024.0)).astype(d[k].dtype)
    return d
def setup_inputs_apart(rng):
    d = setup_inputs(rng)
    f = (10.0 ** rng.permutation(np.linspace(-1.5, 1.5, N))).astype(np.float32).reshape(N, 1, 1)
    for k in ("x", "w"): d[k] = (d[k].astype(np.float32) * f).astype(d[k].dtype)
    return d
def reference(x, w):
    X, W = x.astype(np.float64), w.astype(np.float64)
    s = sum(W[g[0]].T @ np.maximum(sum(X[j] for j in g), 0.0) for g in GROUPS).astype(ml_dtypes.bfloat16)
    return {"y": np.broadcast_to(s, (N,) + s.shape)}

@@ -1,0 +1,130 @@
+from concourse.bass import DstId, RemoteDMATransfer
+from concourse.mybir import AluOpType
+
+F = 512
+M = 4
+P = 2
+WD = F // P
+
+SCRATCH = {
+    "xs": ("sbuf", [128, F], "bfloat16"),
+    "ws": ("sbuf", [128, 128], "bfloat16"),
+    "land": ("sbuf", [128, M * WD], "bfloat16"),
+    "zero": ("sbuf", [128, WD], "bfloat16"),
+    "tt": ("sbuf", [128, WD], "bfloat16"),
+    "pout": ("sbuf", [128, WD], "bfloat16"),
+    "pown": ("sbuf", [128, F], "bfloat16"),
+    "poth": ("sbuf", [128, F], "bfloat16"),
+    "yb": ("sbuf", [128, F], "bfloat16"),
+    "acc0": ("psum", [128, 512], "float32"),
+    "acc1": ("psum", [128, 512], "float32"),
+    "acc2": ("psum", [128, 512], "float32"),
+    "pp": ("psum", [128, 512], "float32"),
+}
+SEMAPHORES = (["ldx", "ldw", "aw", "z", "pe", "sent", "st"]
+              + ["ax%d" % m for m in range(M)]
+              + ["ap%d_%d" % (a, b) for a in range(2) for b in range(P)]
+              + ["v%d" % i for i in range(M + 5)])
+
+
+def rank_program(g, core, T, topo):
+    rank = T.rank_of(core)
+    if rank is None:
+        return
+    groups = T.tables["GROUPS"]
+    gi = [i for i, grp in enumerate(groups) if rank in grp][0]
+    mine = [T.cores[r] for r in groups[gi]]
+    other = [T.cores[r] for r in groups[1 - gi]]
+    s = groups[gi].index(rank)
+    h, q = s % P, s // P
+    S, V = T.sem, g.vector
+    sent = [0]
+
+    def col(a, b=None):
+        return slice(a * WD, ((a + 1) if b is None else b) * WD)
+
+    def engines(src, dst):
+        return bin(topo.mask(src, dst)).count("1")
+
+    def send(src, dsts, sem):
+        mask = topo.mask(core, dsts[0][0])
+        ids = []
+        for c, _ in dsts:
+            mask &= topo.mask(core, c)
+            rid, pid = topo.addr(c, core)
+            ids.append(DstId(rid=rid, pnc=pid))
+        g.remote_dma_fused([RemoteDMATransfer(dst_ids=ids, dma_engine_mask=mask, remote_sem=sem, srcs=[src],
+                                              dsts=[a for _, a in dsts], alu_op=0)], local_sem=S.sent)
+        sent[0] += bin(mask).count("1")
+
+    g.sync.dma_start(T.xs[:], T.x[:]).then_inc(S.ldx, 16)
+    if s == 0:
+        g.scalar.dma_start(T.ws[:], T.w[:]).then_inc(S.ldw, 16)
+    V.memset(T.zero[:], 0.0).then_inc(S.z, 1)
+
+    g.wait_ge(S.ldx, 16)
+    for k in range(1, P + 1):
+        hh = (h + k) % P
+        to = [m for m in range(M) if m != s and m % P == hh]
+        if to:
+            send(T.xs[:, col(hh)], [(mine[m], T.land[:, col(s)]) for m in to], S["ax%d" % s])
+    if s == 0:
+        g.wait_ge(S.ldw, 16)
+        send(T.ws[:], [(mine[m], T.ws[:]) for m in range(1, M)], S.aw)
+
+    order = ([m for m in range(M) if m != s and m % P != h] + [m for m in range(M) if m != s and m % P == h])
+    V.wait_ge(S.ldx, 16)
+    prev = T.xs[:, col(h)]
+    nv = 0
+    for i, m in enumerate(order):
+        V.wait_ge(S["ax%d" % m], engines(mine[m], core))
+        if i:
+            V.wait_ge(S["v%d" % (nv - 1)], 1)
+        acc = T["acc%d" % i][:, 0:WD]
+        V.tensor_tensor(acc, prev, T.land[:, col(m)], AluOpType.add).then_inc(S["v%d" % nv], 1)
+        prev = acc
+        nv += 1
+    V.wait_ge(S.z, 1)
+    V.wait_ge(S["v%d" % (nv - 1)], 1)
+    V.tensor_tensor(T.tt[:], prev, T.zero[:], AluOpType.max).then_inc(S["v%d" % nv], 1)
+
+    g.tensor.wait_ge(S["v%d" % nv], 1)
+    nv += 1
+    if s == 0:
+        g.tensor.wait_ge(S.ldw, 16)
+    else:
+        g.tensor.wait_ge(S.aw, engines(mine[0], core))
+    g.tensor.matmul(T.pp[:, 0:WD], T.ws[:], T.tt[:], True, True).then_inc(S.pe, 1)
+    V.wait_ge(S.pe, 1)
+    V.tensor_copy(T.pout[:], T.pp[:, 0:WD]).then_inc(S["v%d" % nv], 1)
+
+    g.wait_ge(S["v%d" % nv], 1)
+    nv += 1
+    dsts = [(mine[m], T.pown[:, col(h)]) for m in range(M) if m != s and m // P == q]
+    dsts += [(other[m], T.poth[:, col(h)]) for m in range(M) if m // P == q]
+    send(T.pout[:], dsts, S["ap%d_%d" % (gi, h)])
+
+    queues = [g.sync, g.scalar]
+    stores = 0
+    V.wait_ge(S["ap%d_%d" % (1 - gi, h)], engines(other[q * P + h], core))
+    V.tensor_tensor(T.yb[:, col(h)], T.pp[:, 0:WD], T.poth[:, col(h)], AluOpType.add).then_inc(S["v%d" % nv], 1)
+    done = [(col(h), nv)]
+    nv += 1
+    for a, b in ((0, h), (h + 1, P)):
+        if a == b:
+            continue
+        for hh in range(a, b):
+            V.wait_ge(S["ap%d_%d" % (gi, hh)], engines(mine[q * P + hh], core))
+            V.wait_ge(S["ap%d_%d" % (1 - gi, hh)], engines(other[q * P + hh], core))
+        V.tensor_tensor(T.yb[:, col(a, b)], T.pown[:, col(a, b)], T.poth[:, col(a, b)],
+                        AluOpType.add).then_inc(S["v%d" % nv], 1)
+        done.append((col(a, b), nv))
+        nv += 1
+    for c, n in done:
+        Q = queues[stores % 2]
+        Q.wait_ge(S["v%d" % n], 1)
+        Q.dma_start(T.y[:, c], T.yb[:, c]).then_inc(S.st, 16)
+        stores += 1
+
+    g.wait_ge(S.sent, sent[0])
+    g.wait_ge(S.st, 16 * stores)

@@ -1,79 +1,115 @@
 from concourse.bass import DstId, RemoteDMATransfer
-from concourse.mybir import AluOpType
+from concourse.mybir import AluOpType, ActivationFunctionType
 
 F = 512
 M = 4
 P = 2
 WD = F // P
+HW = WD // 2
+NH = 2
+WORLD = 256
 
 SCRATCH = {
     "xs": ("sbuf", [128, F], "bfloat16"),
-    "ws": ("sbuf", [128, 128], "bfloat16"),
+    "w0": ("sbuf", [128, 128], "bfloat16"),
+    "w1": ("sbuf", [128, 128], "bfloat16"),
     "land": ("sbuf", [128, M * WD], "bfloat16"),
-    "zero": ("sbuf", [128, WD], "bfloat16"),
-    "tt": ("sbuf", [128, WD], "bfloat16"),
-    "pout": ("sbuf", [128, WD], "bfloat16"),
-    "pown": ("sbuf", [128, F], "bfloat16"),
-    "poth": ("sbuf", [128, F], "bfloat16"),
+    "tt": ("sbuf", [128, 2 * F], "bfloat16"),
     "yb": ("sbuf", [128, F], "bfloat16"),
     "acc0": ("psum", [128, 512], "float32"),
     "acc1": ("psum", [128, 512], "float32"),
     "acc2": ("psum", [128, 512], "float32"),
-    "pp": ("psum", [128, 512], "float32"),
+    "pye": ("psum", [128, 512], "float32"),
+    "pyl0": ("psum", [128, 512], "float32"),
+    "pyl1": ("psum", [128, 512], "float32"),
 }
-SEMAPHORES = (["ldx", "ldw", "aw", "z", "pe", "sent", "st"]
+SEMAPHORES = (["ldx0", "ldx1", "ldw", "hw", "aw0", "aw1", "pee", "pel0", "pel1", "sc", "cl", "sent", "st"]
               + ["ax%d" % m for m in range(M)]
               + ["ap%d_%d" % (a, b) for a in range(2) for b in range(P)]
-              + ["v%d" % i for i in range(M + 5)])
+              + ["v%d" % i for i in range(6)])
+
+
+def count(mask):
+    return bin(mask).count("1")
+
+
+def w_plan(T, topo, gi):
+    first = T.cores[T.tables["GROUPS"][gi][0]]
+    need = [c for c in T.cores if c != first]
+    near = [c for c in range(WORLD)
+            if topo.host(c) == topo.host(first) and topo.chip(c) == topo.chip(first) and topo.die(c) != topo.die(first)
+            and c not in T.cores and all(topo.may_write(c, d) for d in need)][:NH]
+    return [(c, need[i::len(near)]) for i, c in enumerate(near)]
 
 
 def rank_program(g, core, T, topo):
-    rank = T.rank_of(core)
-    if rank is None:
-        return
     groups = T.tables["GROUPS"]
-    gi = [i for i, grp in enumerate(groups) if rank in grp][0]
-    mine = [T.cores[r] for r in groups[gi]]
-    other = [T.cores[r] for r in groups[1 - gi]]
-    s = groups[gi].index(rank)
-    h, q = s % P, s // P
-    S, V = T.sem, g.vector
+    S, V, PE = T.sem, g.vector, g.tensor
     sent = [0]
 
-    def col(a, b=None):
-        return slice(a * WD, ((a + 1) if b is None else b) * WD)
-
-    def engines(src, dst):
-        return bin(topo.mask(src, dst)).count("1")
-
-    def send(src, dsts, sem):
-        mask = topo.mask(core, dsts[0][0])
+    def send(src, dsts, sem, mask=None):
+        if mask is None:
+            mask = topo.mask(core, dsts[0][0])
+            for c, _ in dsts:
+                mask &= topo.mask(core, c)
         ids = []
         for c, _ in dsts:
-            mask &= topo.mask(core, c)
             rid, pid = topo.addr(c, core)
             ids.append(DstId(rid=rid, pnc=pid))
         g.remote_dma_fused([RemoteDMATransfer(dst_ids=ids, dma_engine_mask=mask, remote_sem=sem, srcs=[src],
                                               dsts=[a for _, a in dsts], alu_op=0)], local_sem=S.sent)
-        sent[0] += bin(mask).count("1")
+        sent[0] += count(mask)
 
-    g.sync.dma_start(T.xs[:], T.x[:]).then_inc(S.ldx, 16)
-    if s == 0:
-        g.scalar.dma_start(T.ws[:], T.w[:]).then_inc(S.ldw, 16)
-    V.memset(T.zero[:], 0.0).then_inc(S.z, 1)
+    rank = T.rank_of(core)
+    if rank is None:
+        for gi in range(len(groups)):
+            first = T.cores[groups[gi][0]]
+            for c, serves in w_plan(T, topo, gi):
+                if c == core:
+                    wb = T["w%d" % gi]
+                    g.wait_ge(S.hw, count(topo.mask(first, core) & ~topo.mask(first, serves[0])))
+                    send(wb[:], [(d, wb[:]) for d in serves], S["aw%d" % gi])
+                    g.wait_ge(S.sent, sent[0])
+        return
 
-    g.wait_ge(S.ldx, 16)
-    for k in range(1, P + 1):
-        hh = (h + k) % P
-        to = [m for m in range(M) if m != s and m % P == hh]
-        if to:
-            send(T.xs[:, col(hh)], [(mine[m], T.land[:, col(s)]) for m in to], S["ax%d" % s])
+    gi = [i for i, grp in enumerate(groups) if rank in grp][0]
+    go = 1 - gi
+    mine = [T.cores[r] for r in groups[gi]]
+    other = [T.cores[r] for r in groups[go]]
+    s = groups[gi].index(rank)
+    h, q = s % P, s // P
+    o = 1 - h
+
+    def col(a):
+        return slice(a * WD, (a + 1) * WD)
+
+    def slot(grp, a):
+        return col(P * grp + a)
+
+    def part(base, c):
+        return slice(base * WD + c * HW, base * WD + (c + 1) * HW)
+
+    def engines(src, dst):
+        return count(topo.mask(src, dst))
+
+    g.sync.dma_start(T.xs[:, col(o)], T.x[:, col(o)]).then_inc(S["ldx%d" % o], 16)
+    g.scalar.dma_start(T.xs[:, col(h)], T.x[:, col(h)]).then_inc(S["ldx%d" % h], 16)
     if s == 0:
+        g.sync.dma_start(T["w%d" % gi][:], T.w[:]).then_inc(S.ldw, 16)
+
+    g.wait_ge(S["ldx%d" % o], 16)
+    send(T.xs[:, col(o)], [(mine[m], T.land[:, col(s)]) for m in range(M) if m % P == o], S["ax%d" % s])
+    if s == 0:
+        plan = w_plan(T, topo, gi)
         g.wait_ge(S.ldw, 16)
-        send(T.ws[:], [(mine[m], T.ws[:]) for m in range(1, M)], S.aw)
+        wb = T["w%d" % gi]
+        send(wb[:], [(c, wb[:]) for c, _ in plan], S.hw,
+             mask=topo.mask(core, plan[0][0]) & ~topo.mask(core, plan[0][1][0]))
+    g.wait_ge(S["ldx%d" % h], 16)
+    send(T.xs[:, col(h)], [(mine[m], T.land[:, col(s)]) for m in range(M) if m != s and m % P == h], S["ax%d" % s])
 
-    order = ([m for m in range(M) if m != s and m % P != h] + [m for m in range(M) if m != s and m % P == h])
-    V.wait_ge(S.ldx, 16)
+    order = [m for m in range(M) if m != s and m % P != h] + [m for m in range(M) if m != s and m % P == h]
+    V.wait_ge(S["ldx%d" % h], 16)
     prev = T.xs[:, col(h)]
     nv = 0
     for i, m in enumerate(order):
@@ -84,47 +120,50 @@ def rank_program(g, core, T, topo):
         V.tensor_tensor(acc, prev, T.land[:, col(m)], AluOpType.add).then_inc(S["v%d" % nv], 1)
         prev = acc
         nv += 1
-    V.wait_ge(S.z, 1)
     V.wait_ge(S["v%d" % (nv - 1)], 1)
-    V.tensor_tensor(T.tt[:], prev, T.zero[:], AluOpType.max).then_inc(S["v%d" % nv], 1)
-
-    g.tensor.wait_ge(S["v%d" % nv], 1)
+    V.tensor_scalar(T.tt[:, slot(gi, h)], prev, 0.0, None, AluOpType.max).then_inc(S["v%d" % nv], 1)
+    own = nv
     nv += 1
-    if s == 0:
-        g.tensor.wait_ge(S.ldw, 16)
-    else:
-        g.tensor.wait_ge(S.aw, engines(mine[0], core))
-    g.tensor.matmul(T.pp[:, 0:WD], T.ws[:], T.tt[:], True, True).then_inc(S.pe, 1)
-    V.wait_ge(S.pe, 1)
-    V.tensor_copy(T.pout[:], T.pp[:, 0:WD]).then_inc(S["v%d" % nv], 1)
 
-    g.wait_ge(S["v%d" % nv], 1)
-    nv += 1
-    dsts = [(mine[m], T.pown[:, col(h)]) for m in range(M) if m != s and m // P == q]
-    dsts += [(other[m], T.poth[:, col(h)]) for m in range(M) if m // P == q]
-    send(T.pout[:], dsts, S["ap%d_%d" % (gi, h)])
+    g.wait_ge(S["v%d" % own], 1)
+    send(T.tt[:, slot(gi, h)],
+         [(other[q * P + h], T.tt[:, slot(gi, h)]), (mine[q * P + o], T.tt[:, slot(gi, h)]),
+          (other[q * P + o], T.tt[:, slot(gi, h)])], S["ap%d_%d" % (gi, h)])
 
-    queues = [g.sync, g.scalar]
-    stores = 0
-    V.wait_ge(S["ap%d_%d" % (1 - gi, h)], engines(other[q * P + h], core))
-    V.tensor_tensor(T.yb[:, col(h)], T.pp[:, 0:WD], T.poth[:, col(h)], AluOpType.add).then_inc(S["v%d" % nv], 1)
-    done = [(col(h), nv)]
-    nv += 1
-    for a, b in ((0, h), (h + 1, P)):
-        if a == b:
-            continue
-        for hh in range(a, b):
-            V.wait_ge(S["ap%d_%d" % (gi, hh)], engines(mine[q * P + hh], core))
-            V.wait_ge(S["ap%d_%d" % (1 - gi, hh)], engines(other[q * P + hh], core))
-        V.tensor_tensor(T.yb[:, col(a, b)], T.pown[:, col(a, b)], T.poth[:, col(a, b)],
-                        AluOpType.add).then_inc(S["v%d" % nv], 1)
-        done.append((col(a, b), nv))
-        nv += 1
-    for c, n in done:
-        Q = queues[stores % 2]
-        Q.wait_ge(S["v%d" % n], 1)
-        Q.dma_start(T.y[:, c], T.yb[:, c]).then_inc(S.st, 16)
-        stores += 1
+    def wait_w(grp):
+        if grp == gi and s == 0:
+            PE.wait_ge(S.ldw, 16)
+        else:
+            passer = [c for c, serves in w_plan(T, topo, grp) if core in serves][0]
+            PE.wait_ge(S["aw%d" % grp], engines(passer, core))
+
+    def wait_t(grp, a):
+        PE.wait_ge(S["ap%d_%d" % (grp, a)], engines((mine if grp == gi else other)[q * P + a], core))
+
+    wait_w(gi)
+    PE.wait_ge(S["v%d" % own], 1)
+    PE.matmul(T.pye[:, 0:WD], T["w%d" % gi][:], T.tt[:, slot(gi, h)], True, False)
+    wait_w(go)
+    wait_t(go, h)
+    PE.matmul(T.pye[:, 0:WD], T["w%d" % go][:], T.tt[:, slot(go, h)], False, True).then_inc(S.pee, 1)
+    wait_t(gi, o)
+    for c in range(2):
+        PE.matmul(T["pyl%d" % c][:, 0:HW], T["w%d" % gi][:], T.tt[:, part(P * gi + o, c)], True, False)
+    wait_t(go, o)
+    for c in range(2):
+        PE.matmul(T["pyl%d" % c][:, 0:HW], T["w%d" % go][:], T.tt[:, part(P * go + o, c)], False,
+                  True).then_inc(S["pel%d" % c], 1)
+
+    g.scalar.wait_ge(S.pee, 1)
+    g.scalar.activation(T.yb[:, col(h)], T.pye[:, 0:WD], ActivationFunctionType.Copy).then_inc(S.sc, 1)
+    g.scalar.wait_ge(S.sc, 1)
+    g.scalar.dma_start(T.y[:, col(h)], T.yb[:, col(h)]).then_inc(S.st, 16)
+    V.wait_ge(S.pel0, 1)
+    V.tensor_copy(T.yb[:, part(o, 0)], T.pyl0[:, 0:HW]).then_inc(S.cl, 1)
+    g.scalar.wait_ge(S.pel1, 1)
+    g.scalar.activation(T.yb[:, part(o, 1)], T.pyl1[:, 0:HW], ActivationFunctionType.Copy).then_inc(S.cl, 1)
+    g.sync.wait_ge(S.cl, 2)
+    g.sync.dma_start(T.y[:, col(o)], T.yb[:, col(o)]).then_inc(S.st, 16)
 
     g.wait_ge(S.sent, sent[0])
-    g.wait_ge(S.st, 16 * stores)
+    g.wait_ge(S.st, 32)

@@ -13,17 +13,21 @@ SCRATCH = {
     "xs": ("sbuf", [128, F], "bfloat16"),
     "w0": ("sbuf", [128, 128], "bfloat16"),
     "w1": ("sbuf", [128, 128], "bfloat16"),
+    "ones": ("sbuf", [128, 128], "bfloat16"),
+    "ident": ("sbuf", [128, 128], "bfloat16"),
     "land": ("sbuf", [128, M * WD], "bfloat16"),
     "tt": ("sbuf", [128, 2 * F], "bfloat16"),
     "yb": ("sbuf", [128, F], "bfloat16"),
     "acc0": ("psum", [128, 512], "float32"),
     "acc1": ("psum", [128, 512], "float32"),
     "acc2": ("psum", [128, 512], "float32"),
+    "accp": ("psum", [128, 512], "float32"),
     "pye": ("psum", [128, 512], "float32"),
     "pyl0": ("psum", [128, 512], "float32"),
     "pyl1": ("psum", [128, 512], "float32"),
 }
-SEMAPHORES = (["ldx0", "ldx1", "ldw", "hw", "aw0", "aw1", "pee", "pel0", "pel1", "sc", "cl", "sent", "st"]
+SEMAPHORES = (["ldx0", "ldx1", "ldw", "hw", "aw0", "aw1", "pee", "pel0", "pel1", "sc", "cl", "sent", "st",
+               "z", "idn", "pes", "sr"]
               + ["ax%d" % m for m in range(M)]
               + ["ap%d_%d" % (a, b) for a in range(2) for b in range(P)]
               + ["v%d" % i for i in range(6)])
@@ -31,6 +35,12 @@ SEMAPHORES = (["ldx0", "ldx1", "ldw", "hw", "aw0", "aw1", "pee", "pel0", "pel1",
 
 def count(mask):
     return bin(mask).count("1")
+
+
+def halves(mask):
+    bits = [i for i in range(mask.bit_length()) if (mask >> i) & 1]
+    k = len(bits) // 2
+    return [sum(1 << i for i in bits[:k]), sum(1 << i for i in bits[k:])]
 
 
 def w_plan(T, topo, gi):
@@ -60,6 +70,9 @@ def rank_program(g, core, T, topo):
                                               dsts=[a for _, a in dsts], alu_op=0)], local_sem=S.sent)
         sent[0] += count(mask)
 
+    def stay(src, near, far):
+        return halves(topo.mask(src, near) & ~topo.mask(src, far))
+
     rank = T.rank_of(core)
     if rank is None:
         for gi in range(len(groups)):
@@ -67,8 +80,10 @@ def rank_program(g, core, T, topo):
             for c, serves in w_plan(T, topo, gi):
                 if c == core:
                     wb = T["w%d" % gi]
-                    g.wait_ge(S.hw, count(topo.mask(first, core) & ~topo.mask(first, serves[0])))
-                    send(wb[:], [(d, wb[:]) for d in serves], S["aw%d" % gi])
+                    g.wait_ge(S.hw, count(stay(first, core, serves[0])[0]))
+                    for k in range(2):
+                        send(wb[:], [(d, wb[:]) for d in serves[k::2]], S["aw%d" % gi],
+                             mask=halves(topo.mask(core, serves[0]))[k])
                     g.wait_ge(S.sent, sent[0])
         return
 
@@ -92,40 +107,59 @@ def rank_program(g, core, T, topo):
     def engines(src, dst):
         return count(topo.mask(src, dst))
 
+    def landed(m):
+        return engines(mine[m], core) if m % P == h else count(halves(topo.mask(mine[m], core))[0])
+
     g.sync.dma_start(T.xs[:, col(o)], T.x[:, col(o)]).then_inc(S["ldx%d" % o], 16)
-    g.scalar.dma_start(T.xs[:, col(h)], T.x[:, col(h)]).then_inc(S["ldx%d" % h], 16)
     if s == 0:
         g.sync.dma_start(T["w%d" % gi][:], T.w[:]).then_inc(S.ldw, 16)
+    g.scalar.wait_ge(S["ldx%d" % o], 16)
+    g.scalar.dma_start(T.xs[:, col(h)], T.x[:, col(h)]).then_inc(S["ldx%d" % h], 16)
+    V.memset(T.ones[:], 1.0).then_inc(S.z, 1)
 
     g.wait_ge(S["ldx%d" % o], 16)
-    send(T.xs[:, col(o)], [(mine[m], T.land[:, col(s)]) for m in range(M) if m % P == o], S["ax%d" % s])
+    for k in range(2):
+        m = ((q + k) % 2) * P + o
+        send(T.xs[:, col(o)], [(mine[m], T.land[:, col(s)])], S["ax%d" % s], mask=halves(topo.mask(core, mine[m]))[k])
     if s == 0:
-        plan = w_plan(T, topo, gi)
         g.wait_ge(S.ldw, 16)
         wb = T["w%d" % gi]
-        send(wb[:], [(c, wb[:]) for c, _ in plan], S.hw,
-             mask=topo.mask(core, plan[0][0]) & ~topo.mask(core, plan[0][1][0]))
+        for k, (c, serves) in enumerate(w_plan(T, topo, gi)):
+            send(wb[:], [(c, wb[:])], S.hw, mask=stay(core, c, serves[0])[k])
     g.wait_ge(S["ldx%d" % h], 16)
     send(T.xs[:, col(h)], [(mine[m], T.land[:, col(s)]) for m in range(M) if m != s and m % P == h], S["ax%d" % s])
+    g.wait_ge(S.z, 1)
+    g.affine_select(T.ident[:], T.ones[:], [[-1, 128]], AluOpType.is_equal, 0.0, 0, 1).then_inc(S.idn, 1)
 
     order = [m for m in range(M) if m != s and m % P != h] + [m for m in range(M) if m != s and m % P == h]
     V.wait_ge(S["ldx%d" % h], 16)
-    prev = T.xs[:, col(h)]
+    prev = T.xs[:, part(h, 0)]
     nv = 0
     for i, m in enumerate(order):
-        V.wait_ge(S["ax%d" % m], engines(mine[m], core))
+        V.wait_ge(S["ax%d" % m], landed(m))
         if i:
             V.wait_ge(S["v%d" % (nv - 1)], 1)
-        acc = T["acc%d" % i][:, 0:WD]
-        V.tensor_tensor(acc, prev, T.land[:, col(m)], AluOpType.add).then_inc(S["v%d" % nv], 1)
+        acc = T["acc%d" % i][:, 0:HW]
+        V.tensor_tensor(acc, prev, T.land[:, part(m, 0)], AluOpType.add).then_inc(S["v%d" % nv], 1)
         prev = acc
         nv += 1
     V.wait_ge(S["v%d" % (nv - 1)], 1)
-    V.tensor_scalar(T.tt[:, slot(gi, h)], prev, 0.0, None, AluOpType.max).then_inc(S["v%d" % nv], 1)
+    V.tensor_scalar(T.tt[:, part(P * gi + h, 0)], prev, 0.0, None, AluOpType.max).then_inc(S["v%d" % nv], 1)
     own = nv
     nv += 1
 
+    PE.wait_ge(S.idn, 1)
+    PE.wait_ge(S["ldx%d" % h], 16)
+    PE.matmul(T.accp[:, 0:HW], T.ident[:], T.xs[:, part(h, 1)], True, False)
+    for i, m in enumerate(order):
+        PE.wait_ge(S["ax%d" % m], landed(m))
+        mm = PE.matmul(T.accp[:, 0:HW], T.ident[:], T.land[:, part(m, 1)], False, i == len(order) - 1)
+    mm.then_inc(S.pes, 1)
+    g.scalar.wait_ge(S.pes, 1)
+    g.scalar.activation(T.tt[:, part(P * gi + h, 1)], T.accp[:, 0:HW], ActivationFunctionType.Relu).then_inc(S.sr, 1)
+
     g.wait_ge(S["v%d" % own], 1)
+    g.wait_ge(S.sr, 1)
     send(T.tt[:, slot(gi, h)],
          [(other[q * P + h], T.tt[:, slot(gi, h)]), (mine[q * P + o], T.tt[:, slot(gi, h)]),
           (other[q * P + o], T.tt[:, slot(gi, h)])], S["ap%d_%d" % (gi, h)])
@@ -135,13 +169,14 @@ def rank_program(g, core, T, topo):
             PE.wait_ge(S.ldw, 16)
         else:
             passer = [c for c, serves in w_plan(T, topo, grp) if core in serves][0]
-            PE.wait_ge(S["aw%d" % grp], engines(passer, core))
+            PE.wait_ge(S["aw%d" % grp], count(halves(topo.mask(passer, core))[0]))
 
     def wait_t(grp, a):
         PE.wait_ge(S["ap%d_%d" % (grp, a)], engines((mine if grp == gi else other)[q * P + a], core))
 
     wait_w(gi)
     PE.wait_ge(S["v%d" % own], 1)
+    PE.wait_ge(S.sr, 1)
     PE.matmul(T.pye[:, 0:WD], T["w%d" % gi][:], T.tt[:, slot(gi, h)], True, False)
     wait_w(go)
     wait_t(go, h)

from concourse.bass import DstId, RemoteDMATransfer
from concourse.mybir import AluOpType, ActivationFunctionType

F = 512
M = 4
P = 2
WD = F // P
HW = WD // 2
NH = 2
WORLD = 256

SCRATCH = {
    "xs": ("sbuf", [128, F], "bfloat16"),
    "w0": ("sbuf", [128, 128], "bfloat16"),
    "w1": ("sbuf", [128, 128], "bfloat16"),
    "ones": ("sbuf", [128, 128], "bfloat16"),
    "ident": ("sbuf", [128, 128], "bfloat16"),
    "land": ("sbuf", [128, M * WD], "bfloat16"),
    "tt": ("sbuf", [128, 2 * F], "bfloat16"),
    "yb": ("sbuf", [128, F], "bfloat16"),
    "acc0": ("psum", [128, 512], "float32"),
    "acc1": ("psum", [128, 512], "float32"),
    "acc2": ("psum", [128, 512], "float32"),
    "accp": ("psum", [128, 512], "float32"),
    "pye": ("psum", [128, 512], "float32"),
    "pyl0": ("psum", [128, 512], "float32"),
    "pyl1": ("psum", [128, 512], "float32"),
}
SEMAPHORES = (["ldx0", "ldx1", "ldw", "hw", "aw0", "aw1", "pee", "pel0", "pel1", "sc", "cl", "sent", "st",
               "z", "idn", "pes", "sr"]
              + ["ax%d" % m for m in range(M)]
              + ["ap%d_%d" % (a, b) for a in range(2) for b in range(P)]
              + ["v%d" % i for i in range(6)])


def count(mask):
    return bin(mask).count("1")


def halves(mask):
    bits = [i for i in range(mask.bit_length()) if (mask >> i) & 1]
    k = len(bits) // 2
    return [sum(1 << i for i in bits[:k]), sum(1 << i for i in bits[k:])]


def w_plan(T, topo, gi):
    first = T.cores[T.tables["GROUPS"][gi][0]]
    need = [c for c in T.cores if c != first]
    near = [c for c in range(WORLD)
            if topo.host(c) == topo.host(first) and topo.chip(c) == topo.chip(first) and topo.die(c) != topo.die(first)
            and c not in T.cores and all(topo.may_write(c, d) for d in need)][:NH]
    return [(c, need[i::len(near)]) for i, c in enumerate(near)]


def rank_program(g, core, T, topo):
    groups = T.tables["GROUPS"]
    S, V, PE = T.sem, g.vector, g.tensor
    sent = [0]

    def send(src, dsts, sem, mask=None):
        if mask is None:
            mask = topo.mask(core, dsts[0][0])
            for c, _ in dsts:
                mask &= topo.mask(core, c)
        ids = []
        for c, _ in dsts:
            rid, pid = topo.addr(c, core)
            ids.append(DstId(rid=rid, pnc=pid))
        g.remote_dma_fused([RemoteDMATransfer(dst_ids=ids, dma_engine_mask=mask, remote_sem=sem, srcs=[src],
                                              dsts=[a for _, a in dsts], alu_op=0)], local_sem=S.sent)
        sent[0] += count(mask)

    def stay(src, near, far):
        return halves(topo.mask(src, near) & ~topo.mask(src, far))

    rank = T.rank_of(core)
    if rank is None:
        for gi in range(len(groups)):
            first = T.cores[groups[gi][0]]
            for c, serves in w_plan(T, topo, gi):
                if c == core:
                    wb = T["w%d" % gi]
                    g.wait_ge(S.hw, count(stay(first, core, serves[0])[0]))
                    for k in range(2):
                        send(wb[:], [(d, wb[:]) for d in serves[k::2]], S["aw%d" % gi],
                             mask=halves(topo.mask(core, serves[0]))[k])
                    g.wait_ge(S.sent, sent[0])
        return

    gi = [i for i, grp in enumerate(groups) if rank in grp][0]
    go = 1 - gi
    mine = [T.cores[r] for r in groups[gi]]
    other = [T.cores[r] for r in groups[go]]
    s = groups[gi].index(rank)
    h, q = s % P, s // P
    o = 1 - h

    def col(a):
        return slice(a * WD, (a + 1) * WD)

    def slot(grp, a):
        return col(P * grp + a)

    def part(base, c):
        return slice(base * WD + c * HW, base * WD + (c + 1) * HW)

    def engines(src, dst):
        return count(topo.mask(src, dst))

    def landed(m):
        return engines(mine[m], core) if m % P == h else count(halves(topo.mask(mine[m], core))[0])

    g.sync.dma_start(T.xs[:, col(o)], T.x[:, col(o)]).then_inc(S["ldx%d" % o], 16)
    if s == 0:
        g.sync.dma_start(T["w%d" % gi][:], T.w[:]).then_inc(S.ldw, 16)
    g.scalar.wait_ge(S["ldx%d" % o], 16)
    g.scalar.dma_start(T.xs[:, col(h)], T.x[:, col(h)]).then_inc(S["ldx%d" % h], 16)
    V.memset(T.ones[:], 1.0).then_inc(S.z, 1)

    g.wait_ge(S["ldx%d" % o], 16)
    for k in range(2):
        m = ((q + k) % 2) * P + o
        send(T.xs[:, col(o)], [(mine[m], T.land[:, col(s)])], S["ax%d" % s], mask=halves(topo.mask(core, mine[m]))[k])
    if s == 0:
        g.wait_ge(S.ldw, 16)
        wb = T["w%d" % gi]
        for k, (c, serves) in enumerate(w_plan(T, topo, gi)):
            send(wb[:], [(c, wb[:])], S.hw, mask=stay(core, c, serves[0])[k])
    g.wait_ge(S["ldx%d" % h], 16)
    send(T.xs[:, col(h)], [(mine[m], T.land[:, col(s)]) for m in range(M) if m != s and m % P == h], S["ax%d" % s])
    g.wait_ge(S.z, 1)
    g.affine_select(T.ident[:], T.ones[:], [[-1, 128]], AluOpType.is_equal, 0.0, 0, 1).then_inc(S.idn, 1)

    order = [m for m in range(M) if m != s and m % P != h] + [m for m in range(M) if m != s and m % P == h]
    V.wait_ge(S["ldx%d" % h], 16)
    prev = T.xs[:, part(h, 0)]
    nv = 0
    for i, m in enumerate(order):
        V.wait_ge(S["ax%d" % m], landed(m))
        if i:
            V.wait_ge(S["v%d" % (nv - 1)], 1)
        acc = T["acc%d" % i][:, 0:HW]
        V.tensor_tensor(acc, prev, T.land[:, part(m, 0)], AluOpType.add).then_inc(S["v%d" % nv], 1)
        prev = acc
        nv += 1
    V.wait_ge(S["v%d" % (nv - 1)], 1)
    V.tensor_scalar(T.tt[:, part(P * gi + h, 0)], prev, 0.0, None, AluOpType.max).then_inc(S["v%d" % nv], 1)
    own = nv
    nv += 1

    PE.wait_ge(S.idn, 1)
    PE.wait_ge(S["ldx%d" % h], 16)
    PE.matmul(T.accp[:, 0:HW], T.ident[:], T.xs[:, part(h, 1)], True, False)
    for i, m in enumerate(order):
        PE.wait_ge(S["ax%d" % m], landed(m))
        mm = PE.matmul(T.accp[:, 0:HW], T.ident[:], T.land[:, part(m, 1)], False, i == len(order) - 1)
    mm.then_inc(S.pes, 1)
    g.scalar.wait_ge(S.pes, 1)
    g.scalar.activation(T.tt[:, part(P * gi + h, 1)], T.accp[:, 0:HW], ActivationFunctionType.Relu).then_inc(S.sr, 1)

    g.wait_ge(S["v%d" % own], 1)
    g.wait_ge(S.sr, 1)
    send(T.tt[:, slot(gi, h)],
         [(other[q * P + h], T.tt[:, slot(gi, h)]), (mine[q * P + o], T.tt[:, slot(gi, h)]),
          (other[q * P + o], T.tt[:, slot(gi, h)])], S["ap%d_%d" % (gi, h)])

    def wait_w(grp):
        if grp == gi and s == 0:
            PE.wait_ge(S.ldw, 16)
        else:
            passer = [c for c, serves in w_plan(T, topo, grp) if core in serves][0]
            PE.wait_ge(S["aw%d" % grp], count(halves(topo.mask(passer, core))[0]))

    def wait_t(grp, a):
        PE.wait_ge(S["ap%d_%d" % (grp, a)], engines((mine if grp == gi else other)[q * P + a], core))

    wait_w(gi)
    PE.wait_ge(S["v%d" % own], 1)
    PE.wait_ge(S.sr, 1)
    PE.matmul(T.pye[:, 0:WD], T["w%d" % gi][:], T.tt[:, slot(gi, h)], True, False)
    wait_w(go)
    wait_t(go, h)
    PE.matmul(T.pye[:, 0:WD], T["w%d" % go][:], T.tt[:, slot(go, h)], False, True).then_inc(S.pee, 1)
    wait_t(gi, o)
    for c in range(2):
        PE.matmul(T["pyl%d" % c][:, 0:HW], T["w%d" % gi][:], T.tt[:, part(P * gi + o, c)], True, False)
    wait_t(go, o)
    for c in range(2):
        PE.matmul(T["pyl%d" % c][:, 0:HW], T["w%d" % go][:], T.tt[:, part(P * go + o, c)], False,
                  True).then_inc(S["pel%d" % c], 1)

    g.scalar.wait_ge(S.pee, 1)
    g.scalar.activation(T.yb[:, col(h)], T.pye[:, 0:WD], ActivationFunctionType.Copy).then_inc(S.sc, 1)
    g.scalar.wait_ge(S.sc, 1)
    g.scalar.dma_start(T.y[:, col(h)], T.yb[:, col(h)]).then_inc(S.st, 16)
    V.wait_ge(S.pel0, 1)
    V.tensor_copy(T.yb[:, part(o, 0)], T.pyl0[:, 0:HW]).then_inc(S.cl, 1)
    g.scalar.wait_ge(S.pel1, 1)
    g.scalar.activation(T.yb[:, part(o, 1)], T.pyl1[:, 0:HW], ActivationFunctionType.Copy).then_inc(S.cl, 1)
    g.sync.wait_ge(S.cl, 2)
    g.sync.dma_start(T.y[:, col(o)], T.yb[:, col(o)]).then_inc(S.st, 16)

    g.wait_ge(S.sent, sent[0])
    g.wait_ge(S.st, 32)
